import numpy as np
import ml_dtypes


def mxq(x, axis, fmt="e4m3"):
    dtype, down = {"e4m3": (ml_dtypes.float8_e4m3fn, 7), "e5m2": (ml_dtypes.float8_e5m2, 14)}[fmt]
    v = np.moveaxis(np.asarray(x, np.float32).astype(ml_dtypes.bfloat16).astype(np.float64), axis, -1)
    blocks = v.reshape(v.shape[:-1] + (-1, 32))
    amax = np.abs(blocks).max(-1, keepdims=True)
    byte = np.maximum(np.where(amax > 0, np.frexp(amax)[1] - 1 + 127, 0) - down, 1)
    scale = np.exp2(byte - 127.0)
    codes = (blocks / scale).astype(np.float32).astype(dtype).astype(np.float64)
    return np.moveaxis((codes * scale).reshape(v.shape), -1, axis)


WIDE = False


def mx_kscale(k):
    if not WIDE:
        return np.ones(k)
    levels = np.array([10, -10, 5, -5, 0])
    if k % 512:
        return np.exp2(np.random.permutation(np.resize(levels, k // 32))).repeat(32)
    a = np.empty((k // 512, 16))
    for p in range(k // 512):
        a[p, :8] = np.random.permutation(np.resize(levels, 8))
        for g in range(8):
            far = levels[np.abs(levels - a[p, g]) >= 10]
            a[p, g + 8] = far[np.random.randint(len(far))]
    return np.exp2(a.ravel()).repeat(32)


def f64(x):
    return np.asarray(x).astype(np.float64)


def striped(idx):
    return np.tile(idx.reshape(-1, 16).T, (8, 1)).astype(np.uint16)


def unstriped(offs):
    return offs[:16].T.reshape(-1).astype(np.int64)


def striped8(idx):
    return np.concatenate([x.reshape(-1, 16).T for x in idx]).astype(np.uint16)


def runs(offs, k):
    lists = np.stack([offs[16 * r : 16 * r + 16].T.reshape(-1) for r in range(8)]).astype(np.int64)
    return lists[np.arange(k) % 512 // 64]


def pack_weight(w):
    k, n = w.shape
    w = f64(np.asarray(w, np.float32).astype(ml_dtypes.bfloat16)).reshape(k // 32, 32, n)
    amax = np.abs(w).max(1)
    byte = np.clip(np.where(amax > 0, np.frexp(amax)[1] - 1 + 127 - 7, 1), 1, 254)
    scaled = (w * np.exp2(127.0 - byte)[:, None, :]).reshape(k, n).astype(np.float32)
    words = np.ascontiguousarray(scaled.reshape(k // 512, 128, 4, n).transpose(0, 1, 3, 2)).astype(ml_dtypes.float8_e4m3fn).view(np.uint8)
    return words, np.ascontiguousarray(byte.astype(np.uint8).reshape(k // 512, 16, n))


def unpack_weight(words, scales):
    g, p, n, _ = words.shape
    vals = np.ascontiguousarray(words).view(ml_dtypes.float8_e4m3fn).astype(np.float64) * np.repeat(np.exp2(scales.astype(np.float64) - 127.0), 8, axis=1)[..., None]
    return vals.transpose(0, 1, 3, 2).reshape(g * 512, n)


def sigmoid(v):
    return 1.0 / (1.0 + np.exp(-np.maximum(v, -700.0)))


K, T, S, N, H = 512, 2048, 512, 512, 512


def setup_inputs():
    n = np.random.standard_normal
    s = mx_kscale(K)[:, None]
    u = mx_kscale(H)
    packed_xT = pack_weight(n((K, T)) * s)
    return {
        "x_words": packed_xT[0],
        "x_scales": packed_xT[1],
        "w1": (n((K, H)) / np.sqrt(K) / s).astype(np.float32),
        "w2": (n((K, H)) / np.sqrt(K) / s).astype(np.float32),
        "gn": (np.random.uniform(0.5, 1.5, (H, 1)) * u[:, None]).astype(np.float32),
        "w3": (n((H, N)) / np.sqrt(H) / u[:, None]).astype(np.float32),
        "offs": striped(np.random.permutation(T)[:S]),
        "two": striped(np.random.permutation(T)[:S]),
        "n1": striped8(np.stack([np.random.permutation(S) for _ in range(8)])),
        "n2": striped8(np.stack([np.random.permutation(S) for _ in range(8)])),
        "n3": striped8(np.stack([np.random.permutation(S) for _ in range(8)])),
        "n4": striped8(np.stack([np.random.permutation(S) for _ in range(8)])),
    }


def reference(x_words, x_scales, w1, w2, gn, w3, offs, two, n1, n2, n3, n4):
    xq = unpack_weight(x_words, x_scales)[:, unstriped(offs)]
    y = mxq(f64(w1), 0, "e4m3").T @ xq
    x_two = unpack_weight(x_words, x_scales)[:, unstriped(two)]
    d = mxq(f64(w2), 0, "e4m3").T @ x_two
    z = f64(gn) * ((y + y[np.arange(H)[:, None], runs(n1, H)]) * (sigmoid(d + d[np.arange(H)[:, None], runs(n2, H)])))
    h = mxq(f64(w3), 0, "e4m3").T @ mxq(z, 0, "e4m3")
    st = h * (sigmoid(h[np.arange(N)[:, None], runs(n3, N)]))
    return st - (st[np.arange(N)[:, None], runs(n4, N)])

@@ -1,0 +1,204 @@
+from contextlib import ExitStack
+
+import concourse.mybir as mybir
+
+K, T, S, N, H = 512, 2048, 512, 512, 512
+FLOPS = 2 * S * (K * H + K * H + H * N)
+
+F32 = mybir.dt.float32
+BF16 = mybir.dt.bfloat16
+I32 = mybir.dt.int32
+U32 = mybir.dt.uint32
+U16 = mybir.dt.uint16
+U8 = mybir.dt.uint8
+FP8X4 = mybir.dt.float8_e4m3fn_x4
+ADD = mybir.AluOpType.add
+SUB = mybir.AluOpType.subtract
+MULT = mybir.AluOpType.mult
+COPY = mybir.ActivationFunctionType.Copy
+SIGMOID = mybir.ActivationFunctionType.Sigmoid
+
+P = 128
+PACK = 4
+WINDOW = 2 * S
+HALVES = 2
+CHUNKS = 2
+
+
+def tile_picked_twltriebhopg_none_p_kernel(tc, x_words, x_scales, w1, w2, gn, w3, offs, two, n1, n2, n3, n4, out):
+    nc = tc.nc
+    with ExitStack() as ctx:
+        lists = ctx.enter_context(tc.tile_pool(name="lists", bufs=1))
+        keep = ctx.enter_context(tc.tile_pool(name="keep", bufs=1))
+        psum = ctx.enter_context(tc.psum_pool(name="psum", bufs=1))
+
+        def load_list(name, src):
+            tile = lists.tile([P, S // 16], U16, name=name)
+            nc.sync.dma_start(tile[:], src)
+            return tile
+
+        def load_half(name, w, h):
+            rows = w.rearrange("(p j) c -> p j c", j=PACK)
+            width = w.shape[1] // HALVES
+            raw = keep.tile([P, PACK, width], F32, name=f"{name}_raw{h}")
+            nc.sync.dma_start(raw[:], rows[:, :, h * width : (h + 1) * width])
+            return raw
+
+        def load_weight(name, w):
+            return [load_half(name, w, h) for h in range(HALVES)]
+
+        def round_weight(name, halves, copies):
+            grouped = keep.tile([P, PACK, P, PACK], BF16, name=f"{name}_grouped", align_bytes=64)
+            width = P // HALVES
+            for h in range(HALVES):
+                copies[h](
+                    grouped[:, :, h * width : (h + 1) * width, :].rearrange("p t m j -> p m j t"),
+                    halves[h][:].rearrange("p j (m t) -> p m j t", t=PACK),
+                )
+            return grouped
+
+        def quantize_weight(name, grouped, codes_name=None):
+            codes = keep.tile([P, PACK * P], U32, name=codes_name or f"{name}_codes", align_bytes=64)
+            scales = keep.tile([P, PACK * P], U8, name=f"{name}_scales", align_bytes=64)
+            nc.vector.quantize_mx(out=codes[:].bitcast(FP8X4), scales=scales[:], in_=grouped[:].rearrange("p t m j -> p (t m j)"))
+            return codes, scales
+
+        def product(bank, weight, t, codes, scales):
+            cols = slice(t * P, (t + 1) * P)
+            nc.tensor.matmul_mx(out=bank, lhsT=weight[0][:, cols].bitcast(FP8X4), lhsT_scale=weight[1][:, cols],
+                                rhs=codes.bitcast(FP8X4), rhs_scale=scales, start=True, stop=True)
+
+        scale_table = keep.tile([P, T], U8, name="scale_table")
+        nc.vector.memset(scale_table[:].bitcast(I32), 0)
+        two_l = load_list("two_l", two)
+        offs_l = load_list("offs_l", offs)
+        warm = keep.tile([P, 8], F32, name="warm")
+        warm_out = keep.tile([P, 8], F32, name="warm_out")
+        nc.gpsimd.memset(warm[:], 0.0)
+        w2_raw = [load_half("w2", w2, 0)]
+        for q in range(4):
+            nc.sync.dma_start(scale_table[32 * q : 32 * q + 4, :].bitcast(I32), x_scales[0, 4 * q : 4 * q + 4, :].bitcast(I32))
+        nc.scalar.activation(warm_out[:], warm[:], SIGMOID)
+        w2_raw.append(load_half("w2", w2, 1))
+        word_table = keep.tile([P, T], I32, name="word_table")
+        nc.sync.dma_start(word_table[:], x_words[0].rearrange("p c r -> p (c r)").bitcast(I32))
+        w1_raw = load_weight("w1", w1)
+        n2_l = load_list("n2_l", n2)
+        gain = keep.tile([P, PACK], F32, name="gain")
+        nc.sync.dma_start(gain[:], gn.rearrange("(p t) o -> p (t o)", t=PACK))
+        n1_l = load_list("n1_l", n1)
+        w3_raw = load_weight("w3", w3)
+        n3_l = load_list("n3_l", n3)
+        n4_l = load_list("n4_l", n4)
+
+        picked = {}
+        for name in ("two", "offs"):
+            picked[name] = (keep.tile([P, S], U32, name=f"{name}_words", align_bytes=64),
+                            keep.tile([P, S], U8, name=f"{name}_bytes", align_bytes=64))
+        nc.vector.tensor_copy(picked["two"][1][:], scale_table[:].indirect(two_l[:]))
+        nc.vector.tensor_copy(picked["offs"][1][:], scale_table[:].indirect(offs_l[:]))
+        w2_q = quantize_weight("w2", round_weight("w2", w2_raw, (nc.scalar.copy, nc.scalar.copy)))
+        nc.vector.tensor_copy(picked["two"][0][:], word_table[:].bitcast(U32).indirect(two_l[:]))
+        nc.vector.tensor_copy(picked["offs"][0][:], word_table[:].bitcast(U32).indirect(offs_l[:]))
+
+        d_banks = [psum.tile([P, S], F32, name=f"bank{t}") for t in range(PACK)]
+        for t in range(PACK):
+            product(d_banks[t][:], w2_q, t, picked["two"][0][:], picked["two"][1][:])
+        w1_q = quantize_weight("w1", round_weight("w1", w1_raw, (nc.scalar.copy, nc.vector.tensor_copy)))
+        y_banks = [psum.tile([P, S], F32, name=f"bank{PACK + t}") for t in range(PACK)]
+        for t in range(PACK):
+            product(y_banks[t][:], w1_q, t, picked["offs"][0][:], picked["offs"][1][:])
+
+        gates = keep.tile([P, PACK, S], F32, name="gates")
+        sums = keep.tile([P, PACK, S], F32, name="sums")
+        d_win, d_twin, y_win, y_twin = {}, {}, [], []
+        for t in (0, 2, 1, 3):
+            win = keep.tile([P, WINDOW], F32, name=f"d_win{t}")
+            twin = keep.tile([P, S], F32, name=f"d_twin{t}")
+            nc.scalar.copy(win[:, :S], d_banks[t][:])
+            if t == 0:
+                nc.scalar.copy(twin[:], d_banks[t][:])
+            elif t != 1:
+                nc.sync.dma_start(twin[:], win[:, :S])
+            d_win[t] = win
+            d_twin[t] = twin
+        for t in range(PACK):
+            win = keep.tile([P, WINDOW], F32, name=f"y_win{t}")
+            twin = keep.tile([P, S], F32, name=f"y_twin{t}", align_bytes=64)
+            nc.scalar.activation(win[:, :S], y_banks[t][:], COPY, scale=gain[:, t : t + 1])
+            nc.sync.dma_start(twin[:], win[:, :S])
+            y_win.append(win)
+            y_twin.append(twin)
+        w3_grouped = round_weight("w3", w3_raw, (nc.scalar.copy, nc.scalar.copy))
+        for t in range(PACK):
+            logit = keep.tile([P, S], F32, name="w1_grouped" if t == 0 else f"logit{t}", align_bytes=64)
+            if t == 1:
+                nc.vector.tensor_copy(d_twin[t][:], d_win[t][:, :S])
+            nc.vector.tensor_tensor(logit[:], d_win[t][:].indirect(n2_l[:]), d_twin[t][:], ADD)
+            nc.scalar.activation(gates[:, t, :], logit[:], SIGMOID)
+        for t in range(PACK):
+            nc.vector.tensor_tensor(sums[:, t, :], y_win[t][:].indirect(n1_l[:]), y_twin[t][:], ADD)
+        w3_q = quantize_weight("w3", w3_grouped, "y_twin2")
+
+        z_codes = keep.tile([P, S], U32, name="z_codes", align_bytes=64)
+        z_scales = keep.tile([P, S], U8, name="z_scales", align_bytes=64)
+        h_win = [keep.tile([P, WINDOW], F32, name=f"h_win{t}") for t in range(PACK)]
+        looked = [keep.tile([P, S], F32, name=f"looked{t}") for t in range(PACK)]
+        width = S // CHUNKS
+
+        def gate(c):
+            cols = slice(c * width, (c + 1) * width)
+            z = keep.tile([P, width, PACK], BF16, name="z", align_bytes=64)
+            nc.vector.tensor_tensor(
+                z[:].rearrange("p (c i) t -> p c t i", i=4),
+                sums[:, :, cols].rearrange("p t (c i) -> p c t i", i=4),
+                gates[:, :, cols].rearrange("p t (c i) -> p c t i", i=4),
+                MULT,
+            )
+            return z
+
+        def project(c, z):
+            cols = slice(c * width, (c + 1) * width)
+            nc.vector.quantize_mx(out=z_codes[:, cols].bitcast(FP8X4), scales=z_scales[:, cols],
+                                  in_=z[:].rearrange("p c t -> p (c t)"))
+            banks = [psum.tile([P, width], F32, name=f"bank{PACK * c + t}") for t in range(PACK)]
+            for t in range(PACK):
+                product(banks[t][:], w3_q, t, z_codes[:, cols], z_scales[:, cols])
+            nc.scalar.activation(h_win[0][:, cols], banks[0][:], SIGMOID)
+            nc.scalar.activation(looked[0][:, cols], banks[0][:], COPY, scale=-1.0)
+            for t in range(1, PACK):
+                nc.scalar.copy(h_win[t][:, cols], banks[t][:])
+
+        for c in range(CHUNKS):
+            project(c, gate(c))
+
+        out_rows = out.rearrange("(p t) s -> p t s", t=PACK)
+        st_win = [keep.tile([P, WINDOW], F32, name=f"st_win{t}") for t in range(PACK)]
+        st_twin = [keep.tile([P, S], F32, name=f"st_twin{t}") for t in range(PACK)]
+
+        def look_up(t):
+            nc.scalar.activation(looked[t][:], h_win[t][:].indirect(n3_l[:]), SIGMOID)
+
+        def weigh(t):
+            nc.vector.scalar_tensor_tensor(st_win[t][:, :S], h_win[t][:, :S], -1.0, looked[t][:], MULT, MULT)
+
+        def finish(t):
+            res = keep.tile([P, S], F32, name=f"res{t}")
+            nc.vector.tensor_tensor(res[:], st_win[t][:].indirect(n4_l[:]), st_twin[t][:], SUB)
+            nc.sync.dma_start(out_rows[:, t, :], res[:])
+
+        nc.vector.tensor_tensor(st_win[0][:, :S], h_win[0][:].indirect(n3_l[:]), looked[0][:], MULT)
+        nc.vector.tensor_copy(st_twin[0][:], st_win[0][:, :S])
+        look_up(1)
+        look_up(2)
+        weigh(1)
+        nc.scalar.copy(st_twin[1][:], st_win[1][:, :S])
+        look_up(3)
+        finish(0)
+        weigh(2)
+        nc.scalar.copy(st_twin[2][:], st_win[2][:, :S])
+        finish(1)
+        weigh(3)
+        nc.scalar.copy(st_twin[3][:], st_win[3][:, :S])
+        finish(2)
+        finish(3)

@@ -30,6 +30,7 @@ def tile_picked_twltriebhopg_none_p_kernel(tc, x_words, x_scales, w1, w2, gn, w3
     with ExitStack() as ctx:
         lists = ctx.enter_context(tc.tile_pool(name="lists", bufs=1))
         keep = ctx.enter_context(tc.tile_pool(name="keep", bufs=1))
+        stage = ctx.enter_context(tc.tile_pool(name="stage", bufs=3))
         psum = ctx.enter_context(tc.psum_pool(name="psum", bufs=1))
 
         def load_list(name, src):
@@ -42,18 +43,18 @@ def tile_picked_twltriebhopg_none_p_kernel(tc, x_words, x_scales, w1, w2, gn, w3
             width = w.shape[1] // HALVES
             raw = keep.tile([P, PACK, width], F32, name=f"{name}_raw{h}")
             nc.sync.dma_start(raw[:], rows[:, :, h * width : (h + 1) * width])
-            return raw
+            return raw[:]
 
         def load_weight(name, w):
             return [load_half(name, w, h) for h in range(HALVES)]
 
         def round_weight(name, halves, copies):
             grouped = keep.tile([P, PACK, P, PACK], BF16, name=f"{name}_grouped", align_bytes=64)
-            width = P // HALVES
-            for h in range(HALVES):
+            width = P // len(halves)
+            for h in range(len(halves)):
                 copies[h](
                     grouped[:, :, h * width : (h + 1) * width, :].rearrange("p t m j -> p m j t"),
-                    halves[h][:].rearrange("p j (m t) -> p m j t", t=PACK),
+                    halves[h].rearrange("p j (m t) -> p m j t", t=PACK),
                 )
             return grouped
 
@@ -82,12 +83,16 @@ def tile_picked_twltriebhopg_none_p_kernel(tc, x_words, x_scales, w1, w2, gn, w3
         w2_raw.append(load_half("w2", w2, 1))
         word_table = keep.tile([P, T], I32, name="word_table")
         nc.sync.dma_start(word_table[:], x_words[0].rearrange("p c r -> p (c r)").bitcast(I32))
-        w1_raw = load_weight("w1", w1)
+        w1_whole = keep.tile([P, PACK, H], F32, name="w1_raw")
+        nc.sync.dma_start(w1_whole[:], w1.rearrange("(p j) c -> p j c", j=PACK))
+        w1_raw = [w1_whole[:]]
         n2_l = load_list("n2_l", n2)
         gain = keep.tile([P, PACK], F32, name="gain")
         nc.sync.dma_start(gain[:], gn.rearrange("(p t) o -> p (t o)", t=PACK))
         n1_l = load_list("n1_l", n1)
-        w3_raw = load_weight("w3", w3)
+        w3_whole = keep.tile([P, PACK, N], F32, name="w3_raw")
+        nc.sync.dma_start(w3_whole[:], w3.rearrange("(p j) c -> p j c", j=PACK))
+        w3_raw = [w3_whole[:, :, h * N // HALVES : (h + 1) * N // HALVES] for h in range(HALVES)]
         n3_l = load_list("n3_l", n3)
         n4_l = load_list("n4_l", n4)
 
@@ -104,7 +109,7 @@ def tile_picked_twltriebhopg_none_p_kernel(tc, x_words, x_scales, w1, w2, gn, w3
         d_banks = [psum.tile([P, S], F32, name=f"bank{t}") for t in range(PACK)]
         for t in range(PACK):
             product(d_banks[t][:], w2_q, t, picked["two"][0][:], picked["two"][1][:])
-        w1_q = quantize_weight("w1", round_weight("w1", w1_raw, (nc.scalar.copy, nc.vector.tensor_copy)))
+        w1_q = quantize_weight("w1", round_weight("w1", w1_raw, (nc.vector.tensor_copy,)))
         y_banks = [psum.tile([P, S], F32, name=f"bank{PACK + t}") for t in range(PACK)]
         for t in range(PACK):
             product(y_banks[t][:], w1_q, t, picked["offs"][0][:], picked["offs"][1][:])
@@ -116,9 +121,9 @@ def tile_picked_twltriebhopg_none_p_kernel(tc, x_words, x_scales, w1, w2, gn, w3
             win = keep.tile([P, WINDOW], F32, name=f"d_win{t}")
             twin = keep.tile([P, S], F32, name=f"d_twin{t}")
             nc.scalar.copy(win[:, :S], d_banks[t][:])
-            if t == 0:
+            if t < 2:
                 nc.scalar.copy(twin[:], d_banks[t][:])
-            elif t != 1:
+            else:
                 nc.sync.dma_start(twin[:], win[:, :S])
             d_win[t] = win
             d_twin[t] = twin
@@ -130,12 +135,10 @@ def tile_picked_twltriebhopg_none_p_kernel(tc, x_words, x_scales, w1, w2, gn, w3
             y_win.append(win)
             y_twin.append(twin)
         w3_grouped = round_weight("w3", w3_raw, (nc.scalar.copy, nc.scalar.copy))
+        logits = keep.tile([P, PACK, S], F32, name="w1_grouped", align_bytes=64)
         for t in range(PACK):
-            logit = keep.tile([P, S], F32, name="w1_grouped" if t == 0 else f"logit{t}", align_bytes=64)
-            if t == 1:
-                nc.vector.tensor_copy(d_twin[t][:], d_win[t][:, :S])
-            nc.vector.tensor_tensor(logit[:], d_win[t][:].indirect(n2_l[:]), d_twin[t][:], ADD)
-            nc.scalar.activation(gates[:, t, :], logit[:], SIGMOID)
+            nc.vector.tensor_tensor(logits[:, t, :], d_win[t][:].indirect(n2_l[:]), d_twin[t][:], ADD)
+            nc.scalar.activation(gates[:, t, :], logits[:, t, :], SIGMOID)
         for t in range(PACK):
             nc.vector.tensor_tensor(sums[:, t, :], y_win[t][:].indirect(n1_l[:]), y_twin[t][:], ADD)
         w3_q = quantize_weight("w3", w3_grouped, "y_twin2")
@@ -144,11 +147,11 @@ def tile_picked_twltriebhopg_none_p_kernel(tc, x_words, x_scales, w1, w2, gn, w3
         z_scales = keep.tile([P, S], U8, name="z_scales", align_bytes=64)
         h_win = [keep.tile([P, WINDOW], F32, name=f"h_win{t}") for t in range(PACK)]
         looked = [keep.tile([P, S], F32, name=f"looked{t}") for t in range(PACK)]
-        width = S // CHUNKS
+        chunks = [slice(0, S // 2), slice(S // 2, 3 * S // 4), slice(3 * S // 4, S)]
+        h_banks = {t: psum.tile([P, S], F32, name=f"bank{t}") for t in range(1, PACK)}
 
-        def gate(c):
-            cols = slice(c * width, (c + 1) * width)
-            z = keep.tile([P, width, PACK], BF16, name="z", align_bytes=64)
+        def gate(cols):
+            z = stage.tile([P, cols.stop - cols.start, PACK], BF16, name="z", align_bytes=64)
             nc.vector.tensor_tensor(
                 z[:].rearrange("p (c i) t -> p c t i", i=4),
                 sums[:, :, cols].rearrange("p t (c i) -> p c t i", i=4),
@@ -157,35 +160,43 @@ def tile_picked_twltriebhopg_none_p_kernel(tc, x_words, x_scales, w1, w2, gn, w3
             )
             return z
 
-        def project(c, z):
-            cols = slice(c * width, (c + 1) * width)
+        def project_first(c, z):
+            cols = chunks[c]
             nc.vector.quantize_mx(out=z_codes[:, cols].bitcast(FP8X4), scales=z_scales[:, cols],
                                   in_=z[:].rearrange("p c t -> p (c t)"))
-            banks = [psum.tile([P, width], F32, name=f"bank{PACK * c + t}") for t in range(PACK)]
-            for t in range(PACK):
-                product(banks[t][:], w3_q, t, z_codes[:, cols], z_scales[:, cols])
-            nc.scalar.activation(h_win[0][:, cols], banks[0][:], SIGMOID)
-            nc.scalar.activation(looked[0][:, cols], banks[0][:], COPY, scale=-1.0)
-            for t in range(1, PACK):
-                nc.scalar.copy(h_win[t][:, cols], banks[t][:])
+            bank = psum.tile([P, cols.stop - cols.start], F32, name=f"bank{PACK + c}")[:]
+            product(bank, w3_q, 0, z_codes[:, cols], z_scales[:, cols])
+            nc.scalar.activation(h_win[0][:, cols], bank, SIGMOID)
+            nc.scalar.activation(looked[0][:, cols], bank, COPY, scale=-1.0)
 
-        for c in range(CHUNKS):
-            project(c, gate(c))
+        z0 = gate(chunks[0])
+        z1 = gate(chunks[1])
+        project_first(0, z0)
+        z2 = gate(chunks[2])
+        project_first(1, z1)
+        project_first(2, z2)
+        for t in range(1, PACK):
+            product(h_banks[t][:], w3_q, t, z_codes[:], z_scales[:])
 
         out_rows = out.rearrange("(p t) s -> p t s", t=PACK)
         st_win = [keep.tile([P, WINDOW], F32, name=f"st_win{t}") for t in range(PACK)]
         st_twin = [keep.tile([P, S], F32, name=f"st_twin{t}") for t in range(PACK)]
 
         def look_up(t):
+            nc.scalar.copy(h_win[t][:, :S], h_banks[t][:])
             nc.scalar.activation(looked[t][:], h_win[t][:].indirect(n3_l[:]), SIGMOID)
 
         def weigh(t):
             nc.vector.scalar_tensor_tensor(st_win[t][:, :S], h_win[t][:, :S], -1.0, looked[t][:], MULT, MULT)
 
-        def finish(t):
-            res = keep.tile([P, S], F32, name=f"res{t}")
-            nc.vector.tensor_tensor(res[:], st_win[t][:].indirect(n4_l[:]), st_twin[t][:], SUB)
-            nc.sync.dma_start(out_rows[:, t, :], res[:])
+        def finish(t, pieces=1):
+            width = S // pieces
+            for i in range(pieces):
+                cols = slice(i * width, (i + 1) * width)
+                res = keep.tile([P, width], F32, name=f"res{t}_{i}")
+                entries = n4_l[:, i * width // 16 : (i + 1) * width // 16]
+                nc.vector.tensor_tensor(res[:], st_win[t][:].indirect(entries), st_twin[t][:, cols], SUB)
+                nc.sync.dma_start(out_rows[:, t, cols], res[:])
 
         nc.vector.tensor_tensor(st_win[0][:, :S], h_win[0][:].indirect(n3_l[:]), looked[0][:], MULT)
         nc.vector.tensor_copy(st_twin[0][:], st_win[0][:, :S])
@@ -201,4 +212,4 @@ def tile_picked_twltriebhopg_none_p_kernel(tc, x_words, x_scales, w1, w2, gn, w3
         weigh(3)
         nc.scalar.copy(st_twin[3][:], st_win[3][:, :S])
         finish(2)
-        finish(3)
+        finish(3, HALVES)

@@ -20,196 +20,210 @@ SIGMOID = mybir.ActivationFunctionType.Sigmoid
 
 P = 128
 PACK = 4
+QUADRANT = 32
+SCALE_ROWS = 4
+GROUP = 16
+LINE = 4
+MX_ALIGN = 64
 WINDOW = 2 * S
 HALVES = 2
-CHUNKS = 2
+SCALAR_TWINS = 2
+D_COPY_ORDER = (0, 2, 1, 3)
+Z_STRETCHES = (slice(0, S // 2), slice(S // 2, 3 * S // 4), slice(3 * S // 4, S))
 
 
-def tile_picked_twltriebhopg_none_p_kernel(tc, x_words, x_scales, w1, w2, gn, w3, offs, two, n1, n2, n3, n4, out):
+def tile_picked_twltriebhopg_none_p_kernel(
+    tc, x_words, x_scales, w1, w2, gn, w3, offs, two, n1, n2, n3, n4, out
+):
     nc = tc.nc
     with ExitStack() as ctx:
         lists = ctx.enter_context(tc.tile_pool(name="lists", bufs=1))
         keep = ctx.enter_context(tc.tile_pool(name="keep", bufs=1))
-        stage = ctx.enter_context(tc.tile_pool(name="stage", bufs=3))
         psum = ctx.enter_context(tc.psum_pool(name="psum", bufs=1))
 
         def load_list(name, src):
-            tile = lists.tile([P, S // 16], U16, name=name)
+            tile = lists.tile([P, S // GROUP], U16, name=name)
             nc.sync.dma_start(tile[:], src)
             return tile
 
-        def load_half(name, w, h):
-            rows = w.rearrange("(p j) c -> p j c", j=PACK)
-            width = w.shape[1] // HALVES
-            raw = keep.tile([P, PACK, width], F32, name=f"{name}_raw{h}")
-            nc.sync.dma_start(raw[:], rows[:, :, h * width : (h + 1) * width])
-            return raw[:]
+        def load_weight(name, w, cols):
+            raw = keep.tile([P, PACK, cols.stop - cols.start], F32, name=name)
+            nc.sync.dma_start(raw[:], w.rearrange("(p j) c -> p j c", j=PACK)[:, :, cols])
+            return raw
 
-        def load_weight(name, w):
-            return [load_half(name, w, h) for h in range(HALVES)]
+        def scalar_round(dst, src):
+            nc.scalar.activation(dst, src, COPY)
 
-        def round_weight(name, halves, copies):
-            grouped = keep.tile([P, PACK, P, PACK], BF16, name=f"{name}_grouped", align_bytes=64)
-            width = P // len(halves)
-            for h in range(len(halves)):
-                copies[h](
-                    grouped[:, :, h * width : (h + 1) * width, :].rearrange("p t m j -> p m j t"),
-                    halves[h].rearrange("p j (m t) -> p m j t", t=PACK),
+        def round_weight(name, parts, copy):
+            dealt = keep.tile([P, PACK, P, PACK], BF16, name=name, align_bytes=MX_ALIGN)
+            width = P // len(parts)
+            for index, part in enumerate(parts):
+                copy(
+                    dealt[:, :, index * width : (index + 1) * width, :].rearrange("p t m j -> p m j t"),
+                    part.rearrange("p j (m t) -> p m j t", t=PACK),
                 )
-            return grouped
+            return dealt
 
-        def quantize_weight(name, grouped, codes_name=None):
-            codes = keep.tile([P, PACK * P], U32, name=codes_name or f"{name}_codes", align_bytes=64)
-            scales = keep.tile([P, PACK * P], U8, name=f"{name}_scales", align_bytes=64)
-            nc.vector.quantize_mx(out=codes[:].bitcast(FP8X4), scales=scales[:], in_=grouped[:].rearrange("p t m j -> p (t m j)"))
-            return codes, scales
+        def quantize_weight(name, dealt, first, count, codes_tag):
+            codes = keep.tile([P, count * P], U32, name=f"{name}_codes", tag=codes_tag, align_bytes=MX_ALIGN)
+            scales = keep.tile([P, count * P], U8, name=f"{name}_scales", align_bytes=MX_ALIGN)
+            nc.vector.quantize_mx(
+                out=codes[:].bitcast(FP8X4),
+                scales=scales[:],
+                in_=dealt[:, first : first + count].rearrange("p t m j -> p (t m j)"),
+            )
+            return [(codes[:, i * P : (i + 1) * P], scales[:, i * P : (i + 1) * P]) for i in range(count)]
 
-        def product(bank, weight, t, codes, scales):
-            cols = slice(t * P, (t + 1) * P)
-            nc.tensor.matmul_mx(out=bank, lhsT=weight[0][:, cols].bitcast(FP8X4), lhsT_scale=weight[1][:, cols],
-                                rhs=codes.bitcast(FP8X4), rhs_scale=scales, start=True, stop=True)
+        def product(bank, stationary, codes, scales):
+            nc.tensor.matmul_mx(
+                out=bank,
+                lhsT=stationary[0].bitcast(FP8X4),
+                lhsT_scale=stationary[1],
+                rhs=codes.bitcast(FP8X4),
+                rhs_scale=scales,
+                start=True,
+                stop=True,
+            )
 
         scale_table = keep.tile([P, T], U8, name="scale_table")
         nc.vector.memset(scale_table[:].bitcast(I32), 0)
         two_l = load_list("two_l", two)
+        w2_left = load_weight("w2_left", w2, slice(0, H // 2))
+        for q in range(P // QUADRANT):
+            nc.sync.dma_start(
+                scale_table[QUADRANT * q : QUADRANT * q + SCALE_ROWS, :].bitcast(I32),
+                x_scales[0, SCALE_ROWS * q : SCALE_ROWS * (q + 1), :].bitcast(I32),
+            )
         offs_l = load_list("offs_l", offs)
-        warm = keep.tile([P, 8], F32, name="warm")
-        warm_out = keep.tile([P, 8], F32, name="warm_out")
-        nc.gpsimd.memset(warm[:], 0.0)
-        w2_raw = [load_half("w2", w2, 0)]
-        for q in range(4):
-            nc.sync.dma_start(scale_table[32 * q : 32 * q + 4, :].bitcast(I32), x_scales[0, 4 * q : 4 * q + 4, :].bitcast(I32))
-        nc.scalar.activation(warm_out[:], warm[:], SIGMOID)
-        w2_raw.append(load_half("w2", w2, 1))
+        w2_right = load_weight("w2_right", w2, slice(H // 2, H))
         word_table = keep.tile([P, T], I32, name="word_table")
         nc.sync.dma_start(word_table[:], x_words[0].rearrange("p c r -> p (c r)").bitcast(I32))
-        w1_whole = keep.tile([P, PACK, H], F32, name="w1_raw")
-        nc.sync.dma_start(w1_whole[:], w1.rearrange("(p j) c -> p j c", j=PACK))
-        w1_raw = [w1_whole[:]]
+        w1_raw = load_weight("w1_raw", w1, slice(0, H))
         n2_l = load_list("n2_l", n2)
         gain = keep.tile([P, PACK], F32, name="gain")
         nc.sync.dma_start(gain[:], gn.rearrange("(p t) o -> p (t o)", t=PACK))
         n1_l = load_list("n1_l", n1)
-        w3_whole = keep.tile([P, PACK, N], F32, name="w3_raw")
-        nc.sync.dma_start(w3_whole[:], w3.rearrange("(p j) c -> p j c", j=PACK))
-        w3_raw = [w3_whole[:, :, h * N // HALVES : (h + 1) * N // HALVES] for h in range(HALVES)]
+        w3_raw = load_weight("w3_raw", w3, slice(0, N))
         n3_l = load_list("n3_l", n3)
         n4_l = load_list("n4_l", n4)
 
-        picked = {}
-        for name in ("two", "offs"):
-            picked[name] = (keep.tile([P, S], U32, name=f"{name}_words", align_bytes=64),
-                            keep.tile([P, S], U8, name=f"{name}_bytes", align_bytes=64))
-        nc.vector.tensor_copy(picked["two"][1][:], scale_table[:].indirect(two_l[:]))
-        nc.vector.tensor_copy(picked["offs"][1][:], scale_table[:].indirect(offs_l[:]))
-        w2_q = quantize_weight("w2", round_weight("w2", w2_raw, (nc.scalar.copy, nc.scalar.copy)))
-        nc.vector.tensor_copy(picked["two"][0][:], word_table[:].bitcast(U32).indirect(two_l[:]))
-        nc.vector.tensor_copy(picked["offs"][0][:], word_table[:].bitcast(U32).indirect(offs_l[:]))
+        two_words = keep.tile([P, S], U32, name="two_words", align_bytes=MX_ALIGN)
+        two_scales = keep.tile([P, S], U8, name="two_scales", align_bytes=MX_ALIGN)
+        offs_words = keep.tile([P, S], U32, name="offs_words", align_bytes=MX_ALIGN)
+        offs_scales = keep.tile([P, S], U8, name="offs_scales", align_bytes=MX_ALIGN)
+        nc.vector.tensor_copy(two_scales[:], scale_table[:].indirect(two_l[:]))
+        nc.vector.tensor_copy(offs_scales[:], scale_table[:].indirect(offs_l[:]))
+        w2_dealt = round_weight("w2_dealt", [w2_left[:], w2_right[:]], scalar_round)
+        w2_mx = quantize_weight("w2", w2_dealt, 0, PACK, "w2_codes")
+        nc.vector.tensor_copy(two_words[:], word_table[:].bitcast(U32).indirect(two_l[:]))
+        nc.vector.tensor_copy(offs_words[:], word_table[:].bitcast(U32).indirect(offs_l[:]))
 
-        d_banks = [psum.tile([P, S], F32, name=f"bank{t}") for t in range(PACK)]
+        d_banks = [psum.tile([P, S], F32, name=f"d_bank{t}", tag=f"bank{t}") for t in range(PACK)]
         for t in range(PACK):
-            product(d_banks[t][:], w2_q, t, picked["two"][0][:], picked["two"][1][:])
-        w1_q = quantize_weight("w1", round_weight("w1", w1_raw, (nc.vector.tensor_copy,)))
-        y_banks = [psum.tile([P, S], F32, name=f"bank{PACK + t}") for t in range(PACK)]
+            product(d_banks[t][:], w2_mx[t], two_words[:], two_scales[:])
+        w1_dealt = round_weight("w1_dealt", [w1_raw[:]], nc.vector.tensor_copy)
+        w1_mx = quantize_weight("w1", w1_dealt, 0, PACK, "w1_codes")
+        y_banks = [psum.tile([P, S], F32, name=f"y_bank{t}", tag=f"bank{PACK + t}") for t in range(PACK)]
         for t in range(PACK):
-            product(y_banks[t][:], w1_q, t, picked["offs"][0][:], picked["offs"][1][:])
+            product(y_banks[t][:], w1_mx[t], offs_words[:], offs_scales[:])
 
         gates = keep.tile([P, PACK, S], F32, name="gates")
         sums = keep.tile([P, PACK, S], F32, name="sums")
-        d_win, d_twin, y_win, y_twin = {}, {}, [], []
-        for t in (0, 2, 1, 3):
-            win = keep.tile([P, WINDOW], F32, name=f"d_win{t}")
-            twin = keep.tile([P, S], F32, name=f"d_twin{t}")
-            nc.scalar.copy(win[:, :S], d_banks[t][:])
-            if t < 2:
-                nc.scalar.copy(twin[:], d_banks[t][:])
+        d_win, d_twin, y_win, y_twin = {}, {}, {}, {}
+        for t in D_COPY_ORDER:
+            d_win[t] = keep.tile([P, WINDOW], F32, name=f"d_win{t}")
+            d_twin[t] = keep.tile([P, S], F32, name=f"d_twin{t}")
+            nc.scalar.copy(d_win[t][:, :S], d_banks[t][:])
+            if t < SCALAR_TWINS:
+                nc.scalar.copy(d_twin[t][:], d_banks[t][:])
             else:
-                nc.sync.dma_start(twin[:], win[:, :S])
-            d_win[t] = win
-            d_twin[t] = twin
+                nc.sync.dma_start(d_twin[t][:], d_win[t][:, :S])
         for t in range(PACK):
-            win = keep.tile([P, WINDOW], F32, name=f"y_win{t}")
-            twin = keep.tile([P, S], F32, name=f"y_twin{t}", align_bytes=64)
-            nc.scalar.activation(win[:, :S], y_banks[t][:], COPY, scale=gain[:, t : t + 1])
-            nc.sync.dma_start(twin[:], win[:, :S])
-            y_win.append(win)
-            y_twin.append(twin)
-        w3_grouped = round_weight("w3", w3_raw, (nc.scalar.copy, nc.scalar.copy))
-        logits = keep.tile([P, PACK, S], F32, name="w1_grouped", align_bytes=64)
+            y_win[t] = keep.tile([P, WINDOW], F32, name=f"y_win{t}")
+            y_twin[t] = keep.tile([P, S], F32, name=f"y_twin{t}", align_bytes=MX_ALIGN)
+            nc.scalar.activation(y_win[t][:, :S], y_banks[t][:], COPY, scale=gain[:, t : t + 1])
+            nc.sync.dma_start(y_twin[t][:], y_win[t][:, :S])
+        w3_dealt = round_weight("w3_dealt", [w3_raw[:, :, : N // 2], w3_raw[:, :, N // 2 :]], nc.scalar.copy)
+
+        logits = keep.tile([P, PACK, S], F32, name="logits", tag="w1_raw")
         for t in range(PACK):
             nc.vector.tensor_tensor(logits[:, t, :], d_win[t][:].indirect(n2_l[:]), d_twin[t][:], ADD)
             nc.scalar.activation(gates[:, t, :], logits[:, t, :], SIGMOID)
         for t in range(PACK):
             nc.vector.tensor_tensor(sums[:, t, :], y_win[t][:].indirect(n1_l[:]), y_twin[t][:], ADD)
-        w3_q = quantize_weight("w3", w3_grouped, "y_twin2")
 
-        z_codes = keep.tile([P, S], U32, name="z_codes", align_bytes=64)
-        z_scales = keep.tile([P, S], U8, name="z_scales", align_bytes=64)
-        h_win = [keep.tile([P, WINDOW], F32, name=f"h_win{t}") for t in range(PACK)]
-        looked = [keep.tile([P, S], F32, name=f"looked{t}") for t in range(PACK)]
-        chunks = [slice(0, S // 2), slice(S // 2, 3 * S // 4), slice(3 * S // 4, S)]
-        h_banks = {t: psum.tile([P, S], F32, name=f"bank{t}") for t in range(1, PACK)}
+        w3_mx = quantize_weight("w3_tile0", w3_dealt, 0, 1, f"y_twin{PACK - 2}")
+        z_codes = keep.tile([P, S], U32, name="z_codes", align_bytes=MX_ALIGN)
+        z_scales = keep.tile([P, S], U8, name="z_scales", align_bytes=MX_ALIGN)
+        n3_win = [keep.tile([P, WINDOW], F32, name=f"n3_win{t}") for t in range(PACK)]
+        n3_mate = [keep.tile([P, S], F32, name=f"n3_mate{t}") for t in range(PACK)]
+        h_banks = {t: psum.tile([P, S], F32, name=f"h_bank{t}", tag=f"bank{t}") for t in range(1, PACK)}
 
-        def gate(cols):
-            z = stage.tile([P, cols.stop - cols.start, PACK], BF16, name="z", align_bytes=64)
+        def weave_z(c):
+            cols = Z_STRETCHES[c]
+            z = keep.tile([P, cols.stop - cols.start, PACK], BF16, name=f"z{c}", align_bytes=MX_ALIGN)
             nc.vector.tensor_tensor(
-                z[:].rearrange("p (c i) t -> p c t i", i=4),
-                sums[:, :, cols].rearrange("p t (c i) -> p c t i", i=4),
-                gates[:, :, cols].rearrange("p t (c i) -> p c t i", i=4),
+                z[:].rearrange("p (u i) t -> p u t i", i=LINE),
+                sums[:, :, cols].rearrange("p t (u i) -> p u t i", i=LINE),
+                gates[:, :, cols].rearrange("p t (u i) -> p u t i", i=LINE),
                 MULT,
             )
             return z
 
-        def project_first(c, z):
-            cols = chunks[c]
-            nc.vector.quantize_mx(out=z_codes[:, cols].bitcast(FP8X4), scales=z_scales[:, cols],
-                                  in_=z[:].rearrange("p c t -> p (c t)"))
-            bank = psum.tile([P, cols.stop - cols.start], F32, name=f"bank{PACK + c}")[:]
-            product(bank, w3_q, 0, z_codes[:, cols], z_scales[:, cols])
-            nc.scalar.activation(h_win[0][:, cols], bank, SIGMOID)
-            nc.scalar.activation(looked[0][:, cols], bank, COPY, scale=-1.0)
+        def project_tile0(c, z):
+            cols = Z_STRETCHES[c]
+            nc.vector.quantize_mx(
+                out=z_codes[:, cols].bitcast(FP8X4),
+                scales=z_scales[:, cols],
+                in_=z[:].rearrange("p s t -> p (s t)"),
+            )
+            bank = psum.tile([P, cols.stop - cols.start], F32, name=f"h0_bank{c}", tag=f"bank{PACK + c}")
+            product(bank[:], w3_mx[0], z_codes[:, cols], z_scales[:, cols])
+            nc.scalar.activation(n3_win[0][:, cols], bank[:], SIGMOID)
+            nc.scalar.activation(n3_mate[0][:, cols], bank[:], COPY, scale=-1.0)
 
-        z0 = gate(chunks[0])
-        z1 = gate(chunks[1])
-        project_first(0, z0)
-        z2 = gate(chunks[2])
-        project_first(1, z1)
-        project_first(2, z2)
-        for t in range(1, PACK):
-            product(h_banks[t][:], w3_q, t, z_codes[:], z_scales[:])
+        woven = weave_z(0)
+        for c in range(1, len(Z_STRETCHES)):
+            ahead = weave_z(c)
+            project_tile0(c - 1, woven)
+            woven = ahead
+        project_tile0(len(Z_STRETCHES) - 1, woven)
+        w3_mx.extend(quantize_weight("w3_tile1", w3_dealt, 1, 1, "z0"))
+        product(h_banks[1][:], w3_mx[1], z_codes[:], z_scales[:])
+        w3_mx.extend(quantize_weight("w3_tiles23", w3_dealt, 2, 2, "z1"))
+        for t in range(2, PACK):
+            product(h_banks[t][:], w3_mx[t], z_codes[:], z_scales[:])
 
         out_rows = out.rearrange("(p t) s -> p t s", t=PACK)
-        st_win = [keep.tile([P, WINDOW], F32, name=f"st_win{t}") for t in range(PACK)]
-        st_twin = [keep.tile([P, S], F32, name=f"st_twin{t}") for t in range(PACK)]
+        neg_st_win = [keep.tile([P, WINDOW], F32, name=f"neg_st_win{t}") for t in range(PACK)]
+        neg_st_twin = [keep.tile([P, S], F32, name=f"neg_st_twin{t}") for t in range(PACK)]
 
-        def look_up(t):
-            nc.scalar.copy(h_win[t][:, :S], h_banks[t][:])
-            nc.scalar.activation(looked[t][:], h_win[t][:].indirect(n3_l[:]), SIGMOID)
+        def look_up_gate(t):
+            nc.scalar.copy(n3_win[t][:, :S], h_banks[t][:])
+            nc.scalar.activation(n3_mate[t][:], n3_win[t][:].indirect(n3_l[:]), SIGMOID)
 
         def weigh(t):
-            nc.vector.scalar_tensor_tensor(st_win[t][:, :S], h_win[t][:, :S], -1.0, looked[t][:], MULT, MULT)
+            nc.vector.scalar_tensor_tensor(neg_st_win[t][:, :S], n3_win[t][:, :S], -1.0, n3_mate[t][:], MULT, MULT)
 
-        def finish(t, pieces=1):
+        def finish(t, pieces):
             width = S // pieces
             for i in range(pieces):
                 cols = slice(i * width, (i + 1) * width)
-                res = keep.tile([P, width], F32, name=f"res{t}_{i}")
-                entries = n4_l[:, i * width // 16 : (i + 1) * width // 16]
-                nc.vector.tensor_tensor(res[:], st_win[t][:].indirect(entries), st_twin[t][:, cols], SUB)
-                nc.sync.dma_start(out_rows[:, t, cols], res[:])
+                entries = n4_l[:, cols.start // GROUP : cols.stop // GROUP]
+                result = keep.tile([P, width], F32, name=f"result{t}_{i}")
+                nc.vector.tensor_tensor(result[:], neg_st_win[t][:].indirect(entries), neg_st_twin[t][:, cols], SUB)
+                nc.sync.dma_start(out_rows[:, t, cols], result[:])
 
-        nc.vector.tensor_tensor(st_win[0][:, :S], h_win[0][:].indirect(n3_l[:]), looked[0][:], MULT)
-        nc.vector.tensor_copy(st_twin[0][:], st_win[0][:, :S])
-        look_up(1)
-        look_up(2)
+        nc.vector.tensor_tensor(neg_st_win[0][:, :S], n3_win[0][:].indirect(n3_l[:]), n3_mate[0][:], MULT)
+        look_up_gate(1)
+        nc.scalar.copy(neg_st_twin[0][:], neg_st_win[0][:, :S])
+        look_up_gate(2)
+        look_up_gate(3)
         weigh(1)
-        nc.scalar.copy(st_twin[1][:], st_win[1][:, :S])
-        look_up(3)
-        finish(0)
-        weigh(2)
-        nc.scalar.copy(st_twin[2][:], st_win[2][:, :S])
-        finish(1)
-        weigh(3)
-        nc.scalar.copy(st_twin[3][:], st_win[3][:, :S])
-        finish(2)
-        finish(3, HALVES)
+        finish(0, 1)
+        nc.vector.tensor_copy(neg_st_twin[1][:], neg_st_win[1][:, :S])
+        for t in range(2, PACK):
+            weigh(t)
+            nc.scalar.copy(neg_st_twin[t][:], neg_st_win[t][:, :S])
+            finish(t - 1, 1)
+        finish(PACK - 1, HALVES)

from contextlib import ExitStack

import concourse.mybir as mybir

K, T, S, N, H = 512, 2048, 512, 512, 512
FLOPS = 2 * S * (K * H + K * H + H * N)

F32 = mybir.dt.float32
BF16 = mybir.dt.bfloat16
I32 = mybir.dt.int32
U32 = mybir.dt.uint32
U16 = mybir.dt.uint16
U8 = mybir.dt.uint8
FP8X4 = mybir.dt.float8_e4m3fn_x4
ADD = mybir.AluOpType.add
SUB = mybir.AluOpType.subtract
MULT = mybir.AluOpType.mult
COPY = mybir.ActivationFunctionType.Copy
SIGMOID = mybir.ActivationFunctionType.Sigmoid

P = 128
PACK = 4
QUADRANT = 32
SCALE_ROWS = 4
GROUP = 16
LINE = 4
MX_ALIGN = 64
WINDOW = 2 * S
HALVES = 2
SCALAR_TWINS = 2
D_COPY_ORDER = (0, 2, 1, 3)
Z_STRETCHES = (slice(0, S // 2), slice(S // 2, 3 * S // 4), slice(3 * S // 4, S))


def tile_picked_twltriebhopg_none_p_kernel(
    tc, x_words, x_scales, w1, w2, gn, w3, offs, two, n1, n2, n3, n4, out
):
    nc = tc.nc
    with ExitStack() as ctx:
        lists = ctx.enter_context(tc.tile_pool(name="lists", bufs=1))
        keep = ctx.enter_context(tc.tile_pool(name="keep", bufs=1))
        psum = ctx.enter_context(tc.psum_pool(name="psum", bufs=1))

        def load_list(name, src):
            tile = lists.tile([P, S // GROUP], U16, name=name)
            nc.sync.dma_start(tile[:], src)
            return tile

        def load_weight(name, w, cols):
            raw = keep.tile([P, PACK, cols.stop - cols.start], F32, name=name)
            nc.sync.dma_start(raw[:], w.rearrange("(p j) c -> p j c", j=PACK)[:, :, cols])
            return raw

        def scalar_round(dst, src):
            nc.scalar.activation(dst, src, COPY)

        def round_weight(name, parts, copy):
            dealt = keep.tile([P, PACK, P, PACK], BF16, name=name, align_bytes=MX_ALIGN)
            width = P // len(parts)
            for index, part in enumerate(parts):
                copy(
                    dealt[:, :, index * width : (index + 1) * width, :].rearrange("p t m j -> p m j t"),
                    part.rearrange("p j (m t) -> p m j t", t=PACK),
                )
            return dealt

        def quantize_weight(name, dealt, first, count, codes_tag):
            codes = keep.tile([P, count * P], U32, name=f"{name}_codes", tag=codes_tag, align_bytes=MX_ALIGN)
            scales = keep.tile([P, count * P], U8, name=f"{name}_scales", align_bytes=MX_ALIGN)
            nc.vector.quantize_mx(
                out=codes[:].bitcast(FP8X4),
                scales=scales[:],
                in_=dealt[:, first : first + count].rearrange("p t m j -> p (t m j)"),
            )
            return [(codes[:, i * P : (i + 1) * P], scales[:, i * P : (i + 1) * P]) for i in range(count)]

        def product(bank, stationary, codes, scales):
            nc.tensor.matmul_mx(
                out=bank,
                lhsT=stationary[0].bitcast(FP8X4),
                lhsT_scale=stationary[1],
                rhs=codes.bitcast(FP8X4),
                rhs_scale=scales,
                start=True,
                stop=True,
            )

        scale_table = keep.tile([P, T], U8, name="scale_table")
        nc.vector.memset(scale_table[:].bitcast(I32), 0)
        two_l = load_list("two_l", two)
        w2_left = load_weight("w2_left", w2, slice(0, H // 2))
        for q in range(P // QUADRANT):
            nc.sync.dma_start(
                scale_table[QUADRANT * q : QUADRANT * q + SCALE_ROWS, :].bitcast(I32),
                x_scales[0, SCALE_ROWS * q : SCALE_ROWS * (q + 1), :].bitcast(I32),
            )
        offs_l = load_list("offs_l", offs)
        w2_right = load_weight("w2_right", w2, slice(H // 2, H))
        word_table = keep.tile([P, T], I32, name="word_table")
        nc.sync.dma_start(word_table[:], x_words[0].rearrange("p c r -> p (c r)").bitcast(I32))
        w1_raw = load_weight("w1_raw", w1, slice(0, H))
        n2_l = load_list("n2_l", n2)
        gain = keep.tile([P, PACK], F32, name="gain")
        nc.sync.dma_start(gain[:], gn.rearrange("(p t) o -> p (t o)", t=PACK))
        n1_l = load_list("n1_l", n1)
        w3_raw = load_weight("w3_raw", w3, slice(0, N))
        n3_l = load_list("n3_l", n3)
        n4_l = load_list("n4_l", n4)

        two_words = keep.tile([P, S], U32, name="two_words", align_bytes=MX_ALIGN)
        two_scales = keep.tile([P, S], U8, name="two_scales", align_bytes=MX_ALIGN)
        offs_words = keep.tile([P, S], U32, name="offs_words", align_bytes=MX_ALIGN)
        offs_scales = keep.tile([P, S], U8, name="offs_scales", align_bytes=MX_ALIGN)
        nc.vector.tensor_copy(two_scales[:], scale_table[:].indirect(two_l[:]))
        nc.vector.tensor_copy(offs_scales[:], scale_table[:].indirect(offs_l[:]))
        w2_dealt = round_weight("w2_dealt", [w2_left[:], w2_right[:]], scalar_round)
        w2_mx = quantize_weight("w2", w2_dealt, 0, PACK, "w2_codes")
        nc.vector.tensor_copy(two_words[:], word_table[:].bitcast(U32).indirect(two_l[:]))
        nc.vector.tensor_copy(offs_words[:], word_table[:].bitcast(U32).indirect(offs_l[:]))

        d_banks = [psum.tile([P, S], F32, name=f"d_bank{t}", tag=f"bank{t}") for t in range(PACK)]
        for t in range(PACK):
            product(d_banks[t][:], w2_mx[t], two_words[:], two_scales[:])
        w1_dealt = round_weight("w1_dealt", [w1_raw[:]], nc.vector.tensor_copy)
        w1_mx = quantize_weight("w1", w1_dealt, 0, PACK, "w1_codes")
        y_banks = [psum.tile([P, S], F32, name=f"y_bank{t}", tag=f"bank{PACK + t}") for t in range(PACK)]
        for t in range(PACK):
            product(y_banks[t][:], w1_mx[t], offs_words[:], offs_scales[:])

        gates = keep.tile([P, PACK, S], F32, name="gates")
        sums = keep.tile([P, PACK, S], F32, name="sums")
        d_win, d_twin, y_win, y_twin = {}, {}, {}, {}
        for t in D_COPY_ORDER:
            d_win[t] = keep.tile([P, WINDOW], F32, name=f"d_win{t}")
            d_twin[t] = keep.tile([P, S], F32, name=f"d_twin{t}")
            nc.scalar.copy(d_win[t][:, :S], d_banks[t][:])
            if t < SCALAR_TWINS:
                nc.scalar.copy(d_twin[t][:], d_banks[t][:])
            else:
                nc.sync.dma_start(d_twin[t][:], d_win[t][:, :S])
        for t in range(PACK):
            y_win[t] = keep.tile([P, WINDOW], F32, name=f"y_win{t}")
            y_twin[t] = keep.tile([P, S], F32, name=f"y_twin{t}", align_bytes=MX_ALIGN)
            nc.scalar.activation(y_win[t][:, :S], y_banks[t][:], COPY, scale=gain[:, t : t + 1])
            nc.sync.dma_start(y_twin[t][:], y_win[t][:, :S])
        w3_dealt = round_weight("w3_dealt", [w3_raw[:, :, : N // 2], w3_raw[:, :, N // 2 :]], nc.scalar.copy)

        logits = keep.tile([P, PACK, S], F32, name="logits", tag="w1_raw")
        for t in range(PACK):
            nc.vector.tensor_tensor(logits[:, t, :], d_win[t][:].indirect(n2_l[:]), d_twin[t][:], ADD)
            nc.scalar.activation(gates[:, t, :], logits[:, t, :], SIGMOID)
        for t in range(PACK):
            nc.vector.tensor_tensor(sums[:, t, :], y_win[t][:].indirect(n1_l[:]), y_twin[t][:], ADD)

        w3_mx = quantize_weight("w3_tile0", w3_dealt, 0, 1, f"y_twin{PACK - 2}")
        z_codes = keep.tile([P, S], U32, name="z_codes", align_bytes=MX_ALIGN)
        z_scales = keep.tile([P, S], U8, name="z_scales", align_bytes=MX_ALIGN)
        n3_win = [keep.tile([P, WINDOW], F32, name=f"n3_win{t}") for t in range(PACK)]
        n3_mate = [keep.tile([P, S], F32, name=f"n3_mate{t}") for t in range(PACK)]
        h_banks = {t: psum.tile([P, S], F32, name=f"h_bank{t}", tag=f"bank{t}") for t in range(1, PACK)}

        def weave_z(c):
            cols = Z_STRETCHES[c]
            z = keep.tile([P, cols.stop - cols.start, PACK], BF16, name=f"z{c}", align_bytes=MX_ALIGN)
            nc.vector.tensor_tensor(
                z[:].rearrange("p (u i) t -> p u t i", i=LINE),
                sums[:, :, cols].rearrange("p t (u i) -> p u t i", i=LINE),
                gates[:, :, cols].rearrange("p t (u i) -> p u t i", i=LINE),
                MULT,
            )
            return z

        def project_tile0(c, z):
            cols = Z_STRETCHES[c]
            nc.vector.quantize_mx(
                out=z_codes[:, cols].bitcast(FP8X4),
                scales=z_scales[:, cols],
                in_=z[:].rearrange("p s t -> p (s t)"),
            )
            bank = psum.tile([P, cols.stop - cols.start], F32, name=f"h0_bank{c}", tag=f"bank{PACK + c}")
            product(bank[:], w3_mx[0], z_codes[:, cols], z_scales[:, cols])
            nc.scalar.activation(n3_win[0][:, cols], bank[:], SIGMOID)
            nc.scalar.activation(n3_mate[0][:, cols], bank[:], COPY, scale=-1.0)

        woven = weave_z(0)
        for c in range(1, len(Z_STRETCHES)):
            ahead = weave_z(c)
            project_tile0(c - 1, woven)
            woven = ahead
        project_tile0(len(Z_STRETCHES) - 1, woven)
        w3_mx.extend(quantize_weight("w3_tile1", w3_dealt, 1, 1, "z0"))
        product(h_banks[1][:], w3_mx[1], z_codes[:], z_scales[:])
        w3_mx.extend(quantize_weight("w3_tiles23", w3_dealt, 2, 2, "z1"))
        for t in range(2, PACK):
            product(h_banks[t][:], w3_mx[t], z_codes[:], z_scales[:])

        out_rows = out.rearrange("(p t) s -> p t s", t=PACK)
        neg_st_win = [keep.tile([P, WINDOW], F32, name=f"neg_st_win{t}") for t in range(PACK)]
        neg_st_twin = [keep.tile([P, S], F32, name=f"neg_st_twin{t}") for t in range(PACK)]

        def look_up_gate(t):
            nc.scalar.copy(n3_win[t][:, :S], h_banks[t][:])
            nc.scalar.activation(n3_mate[t][:], n3_win[t][:].indirect(n3_l[:]), SIGMOID)

        def weigh(t):
            nc.vector.scalar_tensor_tensor(neg_st_win[t][:, :S], n3_win[t][:, :S], -1.0, n3_mate[t][:], MULT, MULT)

        def finish(t, pieces):
            width = S // pieces
            for i in range(pieces):
                cols = slice(i * width, (i + 1) * width)
                entries = n4_l[:, cols.start // GROUP : cols.stop // GROUP]
                result = keep.tile([P, width], F32, name=f"result{t}_{i}")
                nc.vector.tensor_tensor(result[:], neg_st_win[t][:].indirect(entries), neg_st_twin[t][:, cols], SUB)
                nc.sync.dma_start(out_rows[:, t, cols], result[:])

        nc.vector.tensor_tensor(neg_st_win[0][:, :S], n3_win[0][:].indirect(n3_l[:]), n3_mate[0][:], MULT)
        look_up_gate(1)
        nc.scalar.copy(neg_st_twin[0][:], neg_st_win[0][:, :S])
        look_up_gate(2)
        look_up_gate(3)
        weigh(1)
        finish(0, 1)
        nc.vector.tensor_copy(neg_st_twin[1][:], neg_st_win[1][:, :S])
        for t in range(2, PACK):
            weigh(t)
            nc.scalar.copy(neg_st_twin[t][:], neg_st_win[t][:, :S])
            finish(t - 1, 1)
        finish(PACK - 1, HALVES)
